import numpy as np
import ml_dtypes

BF16 = ml_dtypes.bfloat16


def bf(x):
    return np.asarray(x, np.float32).astype(BF16)


def f32(x):
    return np.asarray(x, np.float32)


def f64(x):
    return np.asarray(x).astype(np.float64)


def striped(idx):
    return np.tile(idx.reshape(-1, 16).T, (8, 1))


S, K, M, N, E, Q = 512, 128, 256, 1024, 4, 256


def two_experts():
    first = np.random.permutation(S).reshape(E, S // E)
    return np.concatenate([np.random.permutation(np.concatenate([first[e], first[(e + 1) % E]])) for e in range(E)])


def setup_inputs():
    return {"table": bf(np.random.standard_normal((K, S))), "w": bf(np.random.standard_normal((E, K, M)) / np.sqrt(K)), "b": f32(0.5 * np.random.standard_normal((M, 1))), "offs": striped(two_experts())}


def reference(table, w, b, offs):
    idx = offs[:16].T.reshape(-1)
    x = f64(table)[:, idx]
    y = np.concatenate([f64(w)[e].T @ x[:, e * Q : (e + 1) * Q] for e in range(E)], axis=1)
    return np.maximum(y + f64(b), 0.0)

@@ -1,0 +1,45 @@
+import concourse.mybir as mybir
+
+BF16, F32, U16 = mybir.dt.bfloat16, mybir.dt.float32, mybir.dt.uint16
+ADD, MAX = mybir.AluOpType.add, mybir.AluOpType.max
+RELU = mybir.ActivationFunctionType.Relu
+
+P = 128
+TOKENS = 512
+EXPERTS = 4
+PIECE = 256
+FEATURES = 256
+BLOCKS = FEATURES // P
+OFFSET_COLUMNS = PIECE // 16
+
+FLOPS = 2 * P * FEATURES * EXPERTS * PIECE
+
+
+def tile_gather_matmul_kernel(tc, table, w, b, offs, out):
+    nc = tc.nc
+    with (
+        tc.tile_pool(name="held", bufs=1) as held,
+        tc.tile_pool(name="results", bufs=EXPERTS) as results,
+        tc.psum_pool(name="psum", bufs=EXPERTS * BLOCKS) as psum,
+    ):
+        tokens = held.tile([P, TOKENS], BF16)
+        offsets = held.tile([P, EXPERTS * OFFSET_COLUMNS], U16)
+        weights = held.tile([P, EXPERTS, FEATURES], BF16)
+        bias = held.tile([P, BLOCKS], F32)
+        nc.sync.dma_start(tokens[:], table)
+        nc.sync.dma_start(offsets[:], offs)
+        nc.scalar.dma_start(weights[:], w.rearrange("e k m -> k e m"))
+        nc.scalar.dma_start(bias[:], b.rearrange("(a p) o -> p (a o)", p=P))
+
+        out_blocks = out.rearrange("(a p) n -> p a n", p=P)
+        for e in range(EXPERTS):
+            picked = tokens[:].indirect(offsets[:, e * OFFSET_COLUMNS : (e + 1) * OFFSET_COLUMNS])
+            result = results.tile([P, BLOCKS, PIECE], F32)
+            for a in range(BLOCKS):
+                product = psum.tile([P, PIECE], F32)
+                nc.tensor.matmul(product[:], weights[:, e, a * P : (a + 1) * P], picked, start=True, stop=True)
+                if a == 0:
+                    nc.vector.tensor_scalar(result[:, a, :], product[:], bias[:, a : a + 1], 0.0, op0=ADD, op1=MAX)
+                else:
+                    nc.scalar.activation(result[:, a, :], product[:], RELU, bias=bias[:, a : a + 1])
+            nc.sync.dma_start(out_blocks[:, :, e * PIECE : (e + 1) * PIECE], result[:])

@@ -31,6 +31,11 @@ def tile_gather_matmul_kernel(tc, table, w, b, offs, out):
         nc.scalar.dma_start(weights[:], w.rearrange("e k m -> k e m"))
         nc.scalar.dma_start(bias[:], b.rearrange("(a p) o -> p (a o)", p=P))
 
+        zero = held.tile([P, 1], F32)
+        warmed = held.tile([P, 1], F32)
+        nc.vector.memset(zero[:], 0.0)
+        nc.scalar.activation(warmed[:], zero[:], RELU)
+
         out_blocks = out.rearrange("(a p) n -> p a n", p=P)
         for e in range(EXPERTS):
             picked = tokens[:].indirect(offsets[:, e * OFFSET_COLUMNS : (e + 1) * OFFSET_COLUMNS])

@@ -19,7 +19,7 @@ def tile_gather_matmul_kernel(tc, table, w, b, offs, out):
     nc = tc.nc
     with (
         tc.tile_pool(name="held", bufs=1) as held,
-        tc.tile_pool(name="results", bufs=EXPERTS) as results,
+        tc.tile_pool(name="results", bufs=EXPERTS * BLOCKS) as results,
         tc.psum_pool(name="psum", bufs=EXPERTS * BLOCKS) as psum,
     ):
         tokens = held.tile([P, TOKENS], BF16)
@@ -28,7 +28,9 @@ def tile_gather_matmul_kernel(tc, table, w, b, offs, out):
         bias = held.tile([P, BLOCKS], F32)
         nc.sync.dma_start(tokens[:], table)
         nc.sync.dma_start(offsets[:], offs)
-        nc.scalar.dma_start(weights[:], w.rearrange("e k m -> k e m"))
+        by_feature = w.rearrange("e k m -> k e m")
+        nc.scalar.dma_start(weights[:, 0:1, :], by_feature[:, 0:1, :])
+        nc.scalar.dma_start(weights[:, 1:EXPERTS, :], by_feature[:, 1:EXPERTS, :])
         nc.scalar.dma_start(bias[:], b.rearrange("(a p) o -> p (a o)", p=P))
 
         zero = held.tile([P, 1], F32)
@@ -36,15 +38,16 @@ def tile_gather_matmul_kernel(tc, table, w, b, offs, out):
         nc.vector.memset(zero[:], 0.0)
         nc.scalar.activation(warmed[:], zero[:], RELU)
 
-        out_blocks = out.rearrange("(a p) n -> p a n", p=P)
         for e in range(EXPERTS):
             picked = tokens[:].indirect(offsets[:, e * OFFSET_COLUMNS : (e + 1) * OFFSET_COLUMNS])
-            result = results.tile([P, BLOCKS, PIECE], F32)
             for a in range(BLOCKS):
                 product = psum.tile([P, PIECE], F32)
                 nc.tensor.matmul(product[:], weights[:, e, a * P : (a + 1) * P], picked, start=True, stop=True)
+                result = results.tile([P, PIECE], F32)
+                rows = out[a * P : (a + 1) * P, e * PIECE : (e + 1) * PIECE]
                 if a == 0:
-                    nc.vector.tensor_scalar(result[:, a, :], product[:], bias[:, a : a + 1], 0.0, op0=ADD, op1=MAX)
+                    nc.vector.tensor_scalar(result[:], product[:], bias[:, a : a + 1], 0.0, op0=ADD, op1=MAX)
+                    nc.sync.dma_start(rows, result[:])
                 else:
-                    nc.scalar.activation(result[:, a, :], product[:], RELU, bias=bias[:, a : a + 1])
-            nc.sync.dma_start(out_blocks[:, :, e * PIECE : (e + 1) * PIECE], result[:])
+                    nc.scalar.activation(result[:], product[:], RELU, bias=bias[:, a : a + 1])
+                    nc.scalar.dma_start(rows, result[:])

import concourse.mybir as mybir

BF16, F32, U16 = mybir.dt.bfloat16, mybir.dt.float32, mybir.dt.uint16
ADD, MAX = mybir.AluOpType.add, mybir.AluOpType.max
RELU = mybir.ActivationFunctionType.Relu

P = 128
TOKENS = 512
EXPERTS = 4
PIECE = 256
FEATURES = 256
BLOCKS = FEATURES // P
OFFSET_COLUMNS = PIECE // 16

FLOPS = 2 * P * FEATURES * EXPERTS * PIECE


def tile_gather_matmul_kernel(tc, table, w, b, offs, out):
    nc = tc.nc
    with (
        tc.tile_pool(name="held", bufs=1) as held,
        tc.tile_pool(name="results", bufs=EXPERTS * BLOCKS) as results,
        tc.psum_pool(name="psum", bufs=EXPERTS * BLOCKS) as psum,
    ):
        tokens = held.tile([P, TOKENS], BF16)
        offsets = held.tile([P, EXPERTS * OFFSET_COLUMNS], U16)
        weights = held.tile([P, EXPERTS, FEATURES], BF16)
        bias = held.tile([P, BLOCKS], F32)
        nc.sync.dma_start(tokens[:], table)
        nc.sync.dma_start(offsets[:], offs)
        by_feature = w.rearrange("e k m -> k e m")
        nc.scalar.dma_start(weights[:, 0:1, :], by_feature[:, 0:1, :])
        nc.scalar.dma_start(weights[:, 1:EXPERTS, :], by_feature[:, 1:EXPERTS, :])
        nc.scalar.dma_start(bias[:], b.rearrange("(a p) o -> p (a o)", p=P))

        zero = held.tile([P, 1], F32)
        warmed = held.tile([P, 1], F32)
        nc.vector.memset(zero[:], 0.0)
        nc.scalar.activation(warmed[:], zero[:], RELU)

        for e in range(EXPERTS):
            picked = tokens[:].indirect(offsets[:, e * OFFSET_COLUMNS : (e + 1) * OFFSET_COLUMNS])
            for a in range(BLOCKS):
                product = psum.tile([P, PIECE], F32)
                nc.tensor.matmul(product[:], weights[:, e, a * P : (a + 1) * P], picked, start=True, stop=True)
                result = results.tile([P, PIECE], F32)
                rows = out[a * P : (a + 1) * P, e * PIECE : (e + 1) * PIECE]
                if a == 0:
                    nc.vector.tensor_scalar(result[:], product[:], bias[:, a : a + 1], 0.0, op0=ADD, op1=MAX)
                    nc.sync.dma_start(rows, result[:])
                else:
                    nc.scalar.activation(result[:], product[:], RELU, bias=bias[:, a : a + 1])
                    nc.scalar.dma_start(rows, result[:])
